import numpy as np
import ml_dtypes


def mxq(x, axis, fmt="e4m3"):
    dtype, down = {"e4m3": (ml_dtypes.float8_e4m3fn, 7), "e5m2": (ml_dtypes.float8_e5m2, 14)}[fmt]
    v = np.moveaxis(np.asarray(x, np.float32).astype(ml_dtypes.bfloat16).astype(np.float64), axis, -1)
    blocks = v.reshape(v.shape[:-1] + (-1, 32))
    amax = np.abs(blocks).max(-1, keepdims=True)
    byte = np.maximum(np.where(amax > 0, np.frexp(amax)[1] - 1 + 127, 0) - down, 1)
    scale = np.exp2(byte - 127.0)
    codes = (blocks / scale).astype(np.float32).astype(dtype).astype(np.float64)
    return np.moveaxis((codes * scale).reshape(v.shape), -1, axis)


WIDE = False


def mx_kscale(k):
    if not WIDE:
        return np.ones(k)
    levels = np.array([10, -10, 5, -5, 0])
    if k % 512:
        return np.exp2(np.random.permutation(np.resize(levels, k // 32))).repeat(32)
    a = np.empty((k // 512, 16))
    for p in range(k // 512):
        a[p, :8] = np.random.permutation(np.resize(levels, 8))
        for g in range(8):
            far = levels[np.abs(levels - a[p, g]) >= 10]
            a[p, g + 8] = far[np.random.randint(len(far))]
    return np.exp2(a.ravel()).repeat(32)


def f64(x):
    return np.asarray(x).astype(np.float64)


def striped(idx):
    return np.tile(np.asarray(idx).reshape(-1, 16).T, (8, 1)).astype(np.uint16)


def unstriped(offs):
    return offs[:16].T.reshape(-1).astype(np.int64)


E2M1 = np.array([0.0, 0.5, 1.0, 1.5, 2.0, 3.0, 4.0, 6.0, -0.0, -0.5, -1.0, -1.5, -2.0, -3.0, -4.0, -6.0])


def pack_weight(w, fmt):
    k, n = w.shape
    w = f64(np.asarray(w, np.float32).astype(ml_dtypes.bfloat16)).reshape(k // 32, 32, n)
    amax = np.abs(w).max(1)
    if fmt == "e4m3":
        byte = np.frexp(amax)[1] - 1 + 127 - 7
    else:
        mant, ex = np.frexp(amax / 6.0)
        byte = np.where(mant > 0.5, ex, ex - 1) + 127
    byte = np.clip(np.where(amax > 0, byte, 1), 1, 254)
    scaled = (w * np.exp2(127.0 - byte)[:, None, :]).reshape(k, n).astype(np.float32)
    by_word = np.ascontiguousarray(scaled.reshape(k // 512, 128, 4, n).transpose(0, 1, 3, 2))
    if fmt == "e4m3":
        words = by_word.astype(ml_dtypes.float8_e4m3fn).view(np.uint8)
    else:
        c = by_word.astype(ml_dtypes.float4_e2m1fn).view(np.uint8) & 0xF
        words = (c[..., 0::2] | (c[..., 1::2] << 4)).reshape(k // 512, 128, 2 * n)
    return np.ascontiguousarray(words), np.ascontiguousarray(byte.astype(np.uint8).reshape(k // 512, 16, n))


def unpack_weight(words, scales, fmt):
    g, _, n = scales.shape
    words = np.ascontiguousarray(words).reshape(g, 128, n, -1)
    if fmt == "e4m3":
        vals = words.view(ml_dtypes.float8_e4m3fn).astype(np.float64)
    else:
        nib = np.empty((g, 128, n, 4), np.uint8)
        nib[..., 0::2] = words & 0xF
        nib[..., 1::2] = words >> 4
        vals = E2M1[nib]
    vals = vals * np.repeat(np.exp2(scales.astype(np.float64) - 127.0), 8, axis=1)[..., None]
    return vals.transpose(0, 1, 3, 2).reshape(g * 512, n)


def sigmoid(v):
    return 1.0 / (1.0 + np.exp(-v))


K, R, F, T, J, U = 512, 128, 512, 2048, 512, 1024


def setup_inputs():
    n = np.random.standard_normal
    idx = np.random.permutation(T)[:J]
    idx2 = np.random.permutation(U)[:J]
    fk = mx_kscale(K)
    ff = mx_kscale(F)
    tabp = pack_weight(n((K, T)) / fk[:, None], "e4m3")
    dtabp = pack_weight(n((K, T)) / fk[:, None], "e4m3")
    return {
        "tab_words": tabp[0],
        "tab_scales": tabp[1],
        "w1": (n((K, R)) * 1 / np.sqrt(K) * fk[:, None]).astype(np.float32),
        "w2": (n((K, R)) * 1 / np.sqrt(K) * fk[:, None]).astype(np.float32),
        "bias": (np.random.uniform(-0.5, 0.5, (R, 1))).astype(np.float32),
        "carry": (n((R, U)) * 0.7).astype(np.float32),
        "wo": (n((F, R)) * 1 / np.sqrt(F) * ff[:, None]).astype(np.float32),
        "dy": (n((F, J)) / ff[:, None]).astype(np.float32),
        "dtab_words": dtabp[0],
        "dtab_scales": dtabp[1],
        "og": (np.random.uniform(0.7, 2.0, (R, 1))).astype(np.float32),
        "base": (0.3 * n((R, J))).astype(np.float32),
        "offs": striped(idx),
        "offs2": striped(idx2),
    }


def reference(tab_words, tab_scales, w1, w2, bias, carry, wo, dy, dtab_words, dtab_scales, og, base, offs, offs2):
    idx = unstriped(offs)
    idx2 = unstriped(offs2)
    tabu = unpack_weight(tab_words, tab_scales, "e4m3")
    dtabu = unpack_weight(dtab_words, dtab_scales, "e4m3")
    w1q = mxq(f64(w1), 0, "e4m3")
    tabidxg = tabu[:, idx]
    a = w1q.T @ tabidxg
    dtabidxg = dtabu[:, idx]
    ta = w1q.T @ dtabidxg
    w2q = mxq(f64(w2), 0, "e4m3")
    b = w2q.T @ tabidxg
    tb = w2q.T @ dtabidxg
    h1 = np.tanh(a)
    gt = sigmoid(b + f64(bias))
    woq = mxq(f64(wo), 0, "e4m3")
    dyq = mxq(f64(dy), 0, "e4m3")
    c0 = woq.T @ dyq
    dgt = c0 * (h1 - f64(carry)[:, idx2])
    xh1 = ta * (1.0 - np.square(h1))
    xgt = tb * gt * (1.0 - gt)
    xdgt = xh1 * c0
    xdb = (xdgt * gt + xgt * dgt) * (1.0 - gt) + xgt * (-1.0) * dgt * gt
    y = xdb * f64(og) + f64(base)
    return y

@@ -1,0 +1,178 @@
+from contextlib import ExitStack
+
+import concourse.mybir as mybir
+
+K, R, F, T, J, U = 512, 128, 512, 2048, 512, 1024
+FLOPS = 5 * 2 * 512 * R * J
+
+F32 = mybir.dt.float32
+BF16 = mybir.dt.bfloat16
+I32 = mybir.dt.int32
+U32 = mybir.dt.uint32
+U16 = mybir.dt.uint16
+U8 = mybir.dt.uint8
+FP8X4 = mybir.dt.float8_e4m3fn_x4
+ALU = mybir.AluOpType
+ACT = mybir.ActivationFunctionType
+
+P = 128
+PACK = 4
+HALF = J // 2
+DTAB_ROW = 4
+
+
+def interleave(engine_copy, grouped, raw):
+    engine_copy(
+        out=grouped.rearrange("p (c i t) -> p c t i", i=4, t=PACK),
+        in_=raw.rearrange("p t (c i) -> p c t i", i=4),
+    )
+
+
+def tile_attend_hvcarrymix_kernel(tc, tab_words, tab_scales, w1, w2, bias, carry, wo, dy, dtab_words, dtab_scales, og, base, offs, offs2, out):
+    nc = tc.nc
+    with ExitStack() as ctx:
+        sb = ctx.enter_context(tc.tile_pool(name="sb", bufs=1))
+        ps = ctx.enter_context(tc.psum_pool(name="ps", bufs=1))
+
+        def tile(name, shape, dtype, tag=None):
+            return sb.tile(shape, dtype, name=name, tag=tag or name, align_bytes=64)
+
+        offs_t = tile("offs_t", [P, J // 16], U16)
+        offs2_t = tile("offs2_t", [P, J // 16], U16)
+        tab_s = tile("tab_s", [P, T], U8)
+        w1_raw = tile("w1_raw", [P, PACK, R], F32)
+        w2_raw = tile("w2_raw", [P, PACK, R], F32)
+        bias_t = tile("bias_t", [P, 1], F32)
+        warm = tile("warm", [P, 1], F32)
+        warm_out = tile("warm_out", [P, 1], F32)
+
+        nc.gpsimd.memset(warm[:], 0.0)
+        nc.vector.memset(tab_s[:].bitcast(I32), 0)
+
+        def words(ap):
+            return ap[0].rearrange("p n t -> p (n t)").bitcast(I32)
+
+        def k_rows(ap):
+            return ap.rearrange("(p t) c -> p t c", t=PACK)
+
+        def load_scales(queue, plane, first_row, scales):
+            rows = scales[0].bitcast(I32).rearrange("(q r) n -> r q n", r=4)
+            for r in range(4):
+                queue.dma_start(out=plane[first_row + r : P : 32, :].bitcast(I32), in_=rows[r])
+
+        nc.sync.dma_start(offs_t[:], offs)
+        nc.sync.dma_start(out=w1_raw[:], in_=k_rows(w1))
+        nc.sync.dma_start(out=w2_raw[:], in_=k_rows(w2))
+        nc.sync.dma_start(offs2_t[:], offs2)
+        load_scales(nc.sync, tab_s, 0, tab_scales)
+        nc.gpsimd.dma_start(out=bias_t[:], in_=bias)
+
+        nc.scalar.activation(out=warm_out[:], in_=warm[:], func=ACT.Tanh)
+        tab_w = tile("tab_w", [P, T], U32, tag="warm")
+        nc.sync.dma_start(out=tab_w[:].bitcast(I32), in_=words(tab_words))
+        dtab_s = tile("dtab_s", [P, T], U8, tag="warm_out")
+        nc.vector.memset(dtab_s[:].bitcast(I32), 0)
+        load_scales(nc.sync, dtab_s, DTAB_ROW, dtab_scales)
+
+        half_bias = tile("half_bias", [P, 1], F32, tag="shared")
+        nc.gpsimd.tensor_scalar(out=half_bias[:], in0=bias_t[:], scalar1=0.5, scalar2=0.0, op0=ALU.mult, op1=ALU.add)
+
+        tab_gs = tile("tab_gs", [P, J], U8)
+        tab_gw = tile("tab_gw", [P, J], U32)
+        nc.vector.tensor_copy(out=tab_gs[:], in_=tab_s[:].indirect(offs_t[:]))
+
+        w12_bf = tile("w12_bf", [P, 2 * R * PACK], BF16)
+        w12_q = tile("w12_q", [P, 2 * R], U32)
+        w12_s = tile("w12_s", [P, 2 * R], U8)
+        interleave(nc.scalar.copy, w12_bf[:, : R * PACK], w1_raw[:])
+        carry_t = tile("carry_t", [P, U], F32, tag="w1_raw")
+        nc.sync.dma_start(out=carry_t[:], in_=carry)
+        interleave(nc.scalar.copy, w12_bf[:, R * PACK :], w2_raw[:])
+        dtab_w = tile("dtab_w", [P, T], U32, tag="w2_raw")
+        nc.sync.dma_start(out=dtab_w[:].bitcast(I32), in_=words(dtab_words))
+        nc.vector.quantize_mx(out=w12_q[:].bitcast(FP8X4), scales=w12_s[:], in_=w12_bf[:])
+
+
+        late_raw = tile("late_raw", [P, (R + J) * PACK + J + 8], F32, tag="w12_bf")
+        wo_raw = late_raw[:, : R * PACK].rearrange("p (t c) -> p t c", t=PACK)
+        dy_raw = [late_raw[:, (R + i * HALF) * PACK : (R + (i + 1) * HALF) * PACK].rearrange("p (t c) -> p t c", t=PACK) for i in range(2)]
+        base_t = late_raw[:, (R + J) * PACK : (R + J) * PACK + J]
+        og_t = late_raw[:, (R + J) * PACK + J : (R + J) * PACK + J + 1]
+        nc.sync.dma_start(out=wo_raw, in_=k_rows(wo))
+        for i in range(2):
+            nc.sync.dma_start(out=dy_raw[i], in_=k_rows(dy)[:, :, i * HALF : (i + 1) * HALF])
+        nc.sync.dma_start(out=og_t, in_=og)
+        nc.sync.dma_start(out=base_t, in_=base)
+
+        nc.vector.tensor_copy(out=tab_gw[:], in_=tab_w[:].indirect(offs_t[:]))
+        dtab_gs = tile("dtab_gs", [P, J], U8, tag="warm")
+        nc.vector.tensor_copy(out=dtab_gs[:], in_=dtab_s[:].indirect(offs_t[:]))
+
+        def product(acc, lhs_q, lhs_s, rhs_q, rhs_s):
+            nc.tensor.matmul_mx(out=acc, lhsT=lhs_q.bitcast(FP8X4), lhsT_scale=lhs_s, rhs=rhs_q.bitcast(FP8X4), rhs_scale=rhs_s, start=True, stop=True)
+
+        a_ps = ps.tile([P, J], F32, name="a_ps")
+        b_ps = ps.tile([P, J], F32, name="b_ps")
+        ta_ps = ps.tile([P, J], F32, name="ta_ps")
+        tb_ps = ps.tile([P, J], F32, name="tb_ps")
+        product(a_ps[:], w12_q[:, :R], w12_s[:, :R], tab_gw[:], tab_gs[:])
+        product(b_ps[:], w12_q[:, R:], w12_s[:, R:], tab_gw[:], tab_gs[:])
+
+        h = tile("h", [P, J], F32)
+        t = tile("t", [P, J], F32)
+        h2 = tile("h2", [P, J], F32)
+        t2 = tile("t2", [P, J], F32)
+        nc.scalar.activation(out=h[:], in_=a_ps[:], func=ACT.Tanh)
+        nc.scalar.activation(out=t[:], in_=b_ps[:], func=ACT.Tanh, bias=half_bias[:], scale=0.5)
+        nc.scalar.activation(out=h2[:], in_=h[:], func=ACT.Square)
+        nc.scalar.activation(out=t2[:], in_=t[:], func=ACT.Square, scale=0.5)
+
+        d = tile("d", [P, J], F32)
+        e = tile("e", [P, J], F32)
+        u = tile("u", [P, J], F32)
+        f = tile("f", [P, J], F32)
+        nc.vector.tensor_tensor(out=d[:], in0=carry_t[:].indirect(offs2_t[:]), in1=h[:], op=ALU.subtract)
+        dtab_gw = tile("dtab_gw", [P, J], U32, tag="w1_raw")
+        nc.vector.tensor_copy(out=dtab_gw[:], in_=dtab_w[:].indirect(offs_t[:]))
+        product(ta_ps[:], w12_q[:, :R], w12_s[:, :R], dtab_gw[:], dtab_gs[DTAB_ROW:P, :])
+        product(tb_ps[:], w12_q[:, R:], w12_s[:, R:], dtab_gw[:], dtab_gs[DTAB_ROW:P, :])
+        nc.vector.tensor_tensor(out=e[:], in0=d[:], in1=t[:], op=ALU.mult)
+        nc.vector.scalar_tensor_tensor(out=u[:], in0=h2[:], scalar=-1.0, in1=ta_ps[:], op0=ALU.add, op1=ALU.mult)
+
+        late_bf = sb.tile([P, (R + J) * PACK], BF16, name="late_bf", tag="shared", align_bytes=64)
+        wo_bf = late_bf[:, : R * PACK]
+        wo_q = tile("wo_q", [P, R], U32, tag="w2_raw")
+        wo_s = tile("wo_s", [P, R], U8)
+        interleave(nc.scalar.copy, wo_bf, wo_raw)
+        nc.vector.quantize_mx(out=wo_q[:].bitcast(FP8X4), scales=wo_s[:], in_=wo_bf)
+
+        nc.vector.tensor_tensor(out=f[:], in0=e[:], in1=tb_ps[:], op=ALU.mult)
+
+        c_ps = []
+        for i in range(2):
+            dy_bf = late_bf[:, (R + i * HALF) * PACK : (R + (i + 1) * HALF) * PACK]
+            dy_q = tile("dy_q%d" % i, [P, HALF], U32)
+            dy_s = tile("dy_s%d" % i, [P, HALF], U8)
+            interleave(nc.scalar.copy, dy_bf, dy_raw[i])
+            nc.vector.quantize_mx(out=dy_q[:].bitcast(FP8X4), scales=dy_s[:], in_=dy_bf)
+            acc = ps.tile([P, HALF], F32, name="c_ps%d" % i)
+            product(acc[:], wo_q[:], wo_s[:], dy_q[:], dy_s[:])
+            c_ps.append(acc)
+            if i == 0:
+                v = dy_bf.bitcast(F32)
+                nc.vector.tensor_tensor(out=v, in0=u[:], in1=f[:], op=ALU.subtract)
+            else:
+                z = dy_bf.bitcast(F32)
+
+        for i in range(2):
+            cols = slice(i * HALF, (i + 1) * HALF)
+            nc.vector.scalar_tensor_tensor(out=z[:, cols], in0=t2[:, cols], scalar=-0.25, in1=v[:, cols], op0=ALU.add, op1=ALU.mult)
+        x = [tile("x%d" % i, [P, HALF], F32) for i in range(2)]
+        y = [tile("y%d" % i, [P, HALF], F32) for i in range(2)]
+        for i in range(2):
+            cols = slice(i * HALF, (i + 1) * HALF)
+            nc.vector.scalar_tensor_tensor(out=x[i][:], in0=c_ps[i][:], scalar=og_t, in1=z[:, cols], op0=ALU.mult, op1=ALU.mult)
+        for i in range(2):
+            cols = slice(i * HALF, (i + 1) * HALF)
+            nc.vector.tensor_tensor(out=y[i][:], in0=x[i][:], in1=base_t[:, cols], op=ALU.add)
+            nc.sync.dma_start(out=out[:, cols], in_=y[i][:])

@@ -42,6 +42,7 @@ def tile_attend_hvcarrymix_kernel(tc, tab_words, tab_scales, w1, w2, bias, carry
         tab_s = tile("tab_s", [P, T], U8)
         w1_raw = tile("w1_raw", [P, PACK, R], F32)
         w2_raw = tile("w2_raw", [P, PACK, R], F32)
+        carry_t = tile("carry_t", [P, U], F32)
         bias_t = tile("bias_t", [P, 1], F32)
         warm = tile("warm", [P, 1], F32)
         warm_out = tile("warm_out", [P, 1], F32)
@@ -61,9 +62,10 @@ def tile_attend_hvcarrymix_kernel(tc, tab_words, tab_scales, w1, w2, bias, carry
                 queue.dma_start(out=plane[first_row + r : P : 32, :].bitcast(I32), in_=rows[r])
 
         nc.sync.dma_start(offs_t[:], offs)
+        nc.sync.dma_start(offs2_t[:], offs2)
+        nc.sync.dma_start(out=carry_t[:], in_=carry)
         nc.sync.dma_start(out=w1_raw[:], in_=k_rows(w1))
         nc.sync.dma_start(out=w2_raw[:], in_=k_rows(w2))
-        nc.sync.dma_start(offs2_t[:], offs2)
         load_scales(nc.sync, tab_s, 0, tab_scales)
         nc.gpsimd.dma_start(out=bias_t[:], in_=bias)
 
@@ -77,23 +79,23 @@ def tile_attend_hvcarrymix_kernel(tc, tab_words, tab_scales, w1, w2, bias, carry
         half_bias = tile("half_bias", [P, 1], F32, tag="shared")
         nc.gpsimd.tensor_scalar(out=half_bias[:], in0=bias_t[:], scalar1=0.5, scalar2=0.0, op0=ALU.mult, op1=ALU.add)
 
-        tab_gs = tile("tab_gs", [P, J], U8)
+        carry_g = tile("carry_g", [P, J], F32)
+        nc.vector.tensor_copy(out=carry_g[:], in_=carry_t[:].indirect(offs2_t[:]))
+        tab_gs = tile("tab_gs", [P, J], U8, tag="carry_t")
         tab_gw = tile("tab_gw", [P, J], U32)
         nc.vector.tensor_copy(out=tab_gs[:], in_=tab_s[:].indirect(offs_t[:]))
 
         w12_bf = tile("w12_bf", [P, 2 * R * PACK], BF16)
-        w12_q = tile("w12_q", [P, 2 * R], U32)
+        w12_q = tile("w12_q", [P, 2 * R], U32, tag="tab_s")
         w12_s = tile("w12_s", [P, 2 * R], U8)
         interleave(nc.scalar.copy, w12_bf[:, : R * PACK], w1_raw[:])
-        carry_t = tile("carry_t", [P, U], F32, tag="w1_raw")
-        nc.sync.dma_start(out=carry_t[:], in_=carry)
-        interleave(nc.scalar.copy, w12_bf[:, R * PACK :], w2_raw[:])
-        dtab_w = tile("dtab_w", [P, T], U32, tag="w2_raw")
+        dtab_w = tile("dtab_w", [P, T], U32, tag="w1_raw")
         nc.sync.dma_start(out=dtab_w[:].bitcast(I32), in_=words(dtab_words))
+        interleave(nc.scalar.copy, w12_bf[:, R * PACK :], w2_raw[:])
         nc.vector.quantize_mx(out=w12_q[:].bitcast(FP8X4), scales=w12_s[:], in_=w12_bf[:])
 
 
-        late_raw = tile("late_raw", [P, (R + J) * PACK + J + 8], F32, tag="w12_bf")
+        late_raw = tile("late_raw", [P, (R + J) * PACK + J + 8], F32, tag="w2_raw")
         wo_raw = late_raw[:, : R * PACK].rearrange("p (t c) -> p t c", t=PACK)
         dy_raw = [late_raw[:, (R + i * HALF) * PACK : (R + (i + 1) * HALF) * PACK].rearrange("p (t c) -> p t c", t=PACK) for i in range(2)]
         base_t = late_raw[:, (R + J) * PACK : (R + J) * PACK + J]
@@ -127,21 +129,21 @@ def tile_attend_hvcarrymix_kernel(tc, tab_words, tab_scales, w1, w2, bias, carry
         nc.scalar.activation(out=h2[:], in_=h[:], func=ACT.Square)
         nc.scalar.activation(out=t2[:], in_=t[:], func=ACT.Square, scale=0.5)
 
-        d = tile("d", [P, J], F32)
-        e = tile("e", [P, J], F32)
         u = tile("u", [P, J], F32)
         f = tile("f", [P, J], F32)
-        nc.vector.tensor_tensor(out=d[:], in0=carry_t[:].indirect(offs2_t[:]), in1=h[:], op=ALU.subtract)
-        dtab_gw = tile("dtab_gw", [P, J], U32, tag="w1_raw")
+        dtab_gw = tile("dtab_gw", [P, J], U32, tag="warm_out")
         nc.vector.tensor_copy(out=dtab_gw[:], in_=dtab_w[:].indirect(offs_t[:]))
         product(ta_ps[:], w12_q[:, :R], w12_s[:, :R], dtab_gw[:], dtab_gs[DTAB_ROW:P, :])
         product(tb_ps[:], w12_q[:, R:], w12_s[:, R:], dtab_gw[:], dtab_gs[DTAB_ROW:P, :])
+        d = tile("d", [P, J], F32, tag="w1_raw")
+        e = tile("e", [P, J], F32)
+        nc.vector.tensor_tensor(out=d[:], in0=carry_g[:], in1=h[:], op=ALU.subtract)
         nc.vector.tensor_tensor(out=e[:], in0=d[:], in1=t[:], op=ALU.mult)
         nc.vector.scalar_tensor_tensor(out=u[:], in0=h2[:], scalar=-1.0, in1=ta_ps[:], op0=ALU.add, op1=ALU.mult)
 
         late_bf = sb.tile([P, (R + J) * PACK], BF16, name="late_bf", tag="shared", align_bytes=64)
         wo_bf = late_bf[:, : R * PACK]
-        wo_q = tile("wo_q", [P, R], U32, tag="w2_raw")
+        wo_q = tile("wo_q", [P, R], U32, tag="carry_g")
         wo_s = tile("wo_s", [P, R], U8)
         interleave(nc.scalar.copy, wo_bf, wo_raw)
         nc.vector.quantize_mx(out=wo_q[:].bitcast(FP8X4), scales=wo_s[:], in_=wo_bf)

@@ -44,10 +44,8 @@ def tile_attend_hvcarrymix_kernel(tc, tab_words, tab_scales, w1, w2, bias, carry
         w2_raw = tile("w2_raw", [P, PACK, R], F32)
         carry_t = tile("carry_t", [P, U], F32)
         bias_t = tile("bias_t", [P, 1], F32)
-        warm = tile("warm", [P, 1], F32)
-        warm_out = tile("warm_out", [P, 1], F32)
+        og_t = tile("og_t", [P, 1], F32)
 
-        nc.gpsimd.memset(warm[:], 0.0)
         nc.vector.memset(tab_s[:].bitcast(I32), 0)
 
         def words(ap):
@@ -61,23 +59,24 @@ def tile_attend_hvcarrymix_kernel(tc, tab_words, tab_scales, w1, w2, bias, carry
             for r in range(4):
                 queue.dma_start(out=plane[first_row + r : P : 32, :].bitcast(I32), in_=rows[r])
 
-        nc.sync.dma_start(offs_t[:], offs)
+        nc.scalar.dma_start(out=bias_t[:], in_=bias)
+        nc.scalar.dma_start(out=og_t[:], in_=og)
         nc.sync.dma_start(offs2_t[:], offs2)
+        nc.sync.dma_start(offs_t[:], offs)
         nc.sync.dma_start(out=carry_t[:], in_=carry)
         nc.sync.dma_start(out=w1_raw[:], in_=k_rows(w1))
         nc.sync.dma_start(out=w2_raw[:], in_=k_rows(w2))
         load_scales(nc.sync, tab_s, 0, tab_scales)
-        nc.gpsimd.dma_start(out=bias_t[:], in_=bias)
-
-        nc.scalar.activation(out=warm_out[:], in_=warm[:], func=ACT.Tanh)
-        tab_w = tile("tab_w", [P, T], U32, tag="warm")
-        nc.sync.dma_start(out=tab_w[:].bitcast(I32), in_=words(tab_words))
-        dtab_s = tile("dtab_s", [P, T], U8, tag="warm_out")
-        nc.vector.memset(dtab_s[:].bitcast(I32), 0)
-        load_scales(nc.sync, dtab_s, DTAB_ROW, dtab_scales)
 
         half_bias = tile("half_bias", [P, 1], F32, tag="shared")
-        nc.gpsimd.tensor_scalar(out=half_bias[:], in0=bias_t[:], scalar1=0.5, scalar2=0.0, op0=ALU.mult, op1=ALU.add)
+        gain = tile("gain", [P, 1], F32)
+        nc.vector.tensor_scalar(out=half_bias[:], in0=bias_t[:], scalar1=0.5, scalar2=None, op0=ALU.mult)
+        nc.vector.tensor_scalar(out=gain[:], in0=og_t[:], scalar1=0.25, scalar2=None, op0=ALU.mult)
+        tab_w = tile("tab_w", [P, T], U32, tag="bias_t")
+        nc.sync.dma_start(out=tab_w[:].bitcast(I32), in_=words(tab_words))
+        dtab_s = tile("dtab_s", [P, T], U8, tag="og_t")
+        nc.vector.memset(dtab_s[:].bitcast(I32), 0)
+        load_scales(nc.sync, dtab_s, DTAB_ROW, dtab_scales)
 
         carry_g = tile("carry_g", [P, J], F32)
         nc.vector.tensor_copy(out=carry_g[:], in_=carry_t[:].indirect(offs2_t[:]))
@@ -89,25 +88,25 @@ def tile_attend_hvcarrymix_kernel(tc, tab_words, tab_scales, w1, w2, bias, carry
         w12_q = tile("w12_q", [P, 2 * R], U32, tag="tab_s")
         w12_s = tile("w12_s", [P, 2 * R], U8)
         interleave(nc.scalar.copy, w12_bf[:, : R * PACK], w1_raw[:])
-        dtab_w = tile("dtab_w", [P, T], U32, tag="w1_raw")
-        nc.sync.dma_start(out=dtab_w[:].bitcast(I32), in_=words(dtab_words))
+        wo_raw = tile("wo_raw", [P, PACK, R], F32, tag="w1_raw")
+        nc.sync.dma_start(out=wo_raw[:], in_=k_rows(wo))
         interleave(nc.scalar.copy, w12_bf[:, R * PACK :], w2_raw[:])
+        dtab_w = tile("dtab_w", [P, T], U32, tag="w2_raw")
+        nc.sync.dma_start(out=dtab_w[:].bitcast(I32), in_=words(dtab_words))
         nc.vector.quantize_mx(out=w12_q[:].bitcast(FP8X4), scales=w12_s[:], in_=w12_bf[:])
 
 
-        late_raw = tile("late_raw", [P, (R + J) * PACK + J + 8], F32, tag="w2_raw")
-        wo_raw = late_raw[:, : R * PACK].rearrange("p (t c) -> p t c", t=PACK)
-        dy_raw = [late_raw[:, (R + i * HALF) * PACK : (R + (i + 1) * HALF) * PACK].rearrange("p (t c) -> p t c", t=PACK) for i in range(2)]
-        base_t = late_raw[:, (R + J) * PACK : (R + J) * PACK + J]
-        og_t = late_raw[:, (R + J) * PACK + J : (R + J) * PACK + J + 1]
-        nc.sync.dma_start(out=wo_raw, in_=k_rows(wo))
+        late_raw = tile("late_raw", [P, J * PACK + J], F32, tag="w12_bf")
+        dy_raw = [late_raw[:, i * HALF * PACK : (i + 1) * HALF * PACK].rearrange("p (t c) -> p t c", t=PACK) for i in range(2)]
+        base_t = late_raw[:, J * PACK :]
+        wo_bf = tile("wo_bf", [P, R * PACK], BF16)
+        interleave(nc.scalar.copy, wo_bf[:], wo_raw[:])
         for i in range(2):
             nc.sync.dma_start(out=dy_raw[i], in_=k_rows(dy)[:, :, i * HALF : (i + 1) * HALF])
-        nc.sync.dma_start(out=og_t, in_=og)
         nc.sync.dma_start(out=base_t, in_=base)
 
         nc.vector.tensor_copy(out=tab_gw[:], in_=tab_w[:].indirect(offs_t[:]))
-        dtab_gs = tile("dtab_gs", [P, J], U8, tag="warm")
+        dtab_gs = tile("dtab_gs", [P, J], U8, tag="bias_t")
         nc.vector.tensor_copy(out=dtab_gs[:], in_=dtab_s[:].indirect(offs_t[:]))
 
         def product(acc, lhs_q, lhs_s, rhs_q, rhs_s):
@@ -123,36 +122,34 @@ def tile_attend_hvcarrymix_kernel(tc, tab_words, tab_scales, w1, w2, bias, carry
         h = tile("h", [P, J], F32)
         t = tile("t", [P, J], F32)
         h2 = tile("h2", [P, J], F32)
-        t2 = tile("t2", [P, J], F32)
         nc.scalar.activation(out=h[:], in_=a_ps[:], func=ACT.Tanh)
         nc.scalar.activation(out=t[:], in_=b_ps[:], func=ACT.Tanh, bias=half_bias[:], scale=0.5)
         nc.scalar.activation(out=h2[:], in_=h[:], func=ACT.Square)
-        nc.scalar.activation(out=t2[:], in_=t[:], func=ACT.Square, scale=0.5)
+        t2 = tile("t2", [P, J], F32)
+        nc.scalar.activation(out=t2[:], in_=t[:], func=ACT.Square)
 
         u = tile("u", [P, J], F32)
         f = tile("f", [P, J], F32)
-        dtab_gw = tile("dtab_gw", [P, J], U32, tag="warm_out")
+        dtab_gw = tile("dtab_gw", [P, J], U32, tag="og_t")
         nc.vector.tensor_copy(out=dtab_gw[:], in_=dtab_w[:].indirect(offs_t[:]))
         product(ta_ps[:], w12_q[:, :R], w12_s[:, :R], dtab_gw[:], dtab_gs[DTAB_ROW:P, :])
         product(tb_ps[:], w12_q[:, R:], w12_s[:, R:], dtab_gw[:], dtab_gs[DTAB_ROW:P, :])
-        d = tile("d", [P, J], F32, tag="w1_raw")
-        e = tile("e", [P, J], F32)
-        nc.vector.tensor_tensor(out=d[:], in0=carry_g[:], in1=h[:], op=ALU.subtract)
+        d = tile("d", [P, J], F32)
+        e = tile("e", [P, J], F32, tag="w2_raw")
+        nc.gpsimd.tensor_tensor(out=d[:], in0=carry_g[:], in1=h[:], op=ALU.subtract)
         nc.vector.tensor_tensor(out=e[:], in0=d[:], in1=t[:], op=ALU.mult)
         nc.vector.scalar_tensor_tensor(out=u[:], in0=h2[:], scalar=-1.0, in1=ta_ps[:], op0=ALU.add, op1=ALU.mult)
 
-        late_bf = sb.tile([P, (R + J) * PACK], BF16, name="late_bf", tag="shared", align_bytes=64)
-        wo_bf = late_bf[:, : R * PACK]
-        wo_q = tile("wo_q", [P, R], U32, tag="carry_g")
+        late_bf = tile("late_bf", [P, J * PACK], BF16, tag="shared")
+        wo_q = tile("wo_q", [P, R], U32, tag="d")
         wo_s = tile("wo_s", [P, R], U8)
-        interleave(nc.scalar.copy, wo_bf, wo_raw)
-        nc.vector.quantize_mx(out=wo_q[:].bitcast(FP8X4), scales=wo_s[:], in_=wo_bf)
+        nc.vector.quantize_mx(out=wo_q[:].bitcast(FP8X4), scales=wo_s[:], in_=wo_bf[:])
 
         nc.vector.tensor_tensor(out=f[:], in0=e[:], in1=tb_ps[:], op=ALU.mult)
 
         c_ps = []
         for i in range(2):
-            dy_bf = late_bf[:, (R + i * HALF) * PACK : (R + (i + 1) * HALF) * PACK]
+            dy_bf = late_bf[:, i * HALF * PACK : (i + 1) * HALF * PACK]
             dy_q = tile("dy_q%d" % i, [P, HALF], U32)
             dy_s = tile("dy_s%d" % i, [P, HALF], U8)
             interleave(nc.scalar.copy, dy_bf, dy_raw[i])
@@ -168,12 +165,12 @@ def tile_attend_hvcarrymix_kernel(tc, tab_words, tab_scales, w1, w2, bias, carry
 
         for i in range(2):
             cols = slice(i * HALF, (i + 1) * HALF)
-            nc.vector.scalar_tensor_tensor(out=z[:, cols], in0=t2[:, cols], scalar=-0.25, in1=v[:, cols], op0=ALU.add, op1=ALU.mult)
+            nc.vector.scalar_tensor_tensor(out=z[:, cols], in0=t2[:, cols], scalar=-1.0, in1=v[:, cols], op0=ALU.add, op1=ALU.mult)
         x = [tile("x%d" % i, [P, HALF], F32) for i in range(2)]
         y = [tile("y%d" % i, [P, HALF], F32) for i in range(2)]
         for i in range(2):
             cols = slice(i * HALF, (i + 1) * HALF)
-            nc.vector.scalar_tensor_tensor(out=x[i][:], in0=c_ps[i][:], scalar=og_t, in1=z[:, cols], op0=ALU.mult, op1=ALU.mult)
+            nc.vector.scalar_tensor_tensor(out=x[i][:], in0=c_ps[i][:], scalar=gain[:], in1=z[:, cols], op0=ALU.mult, op1=ALU.mult)
         for i in range(2):
             cols = slice(i * HALF, (i + 1) * HALF)
             nc.vector.tensor_tensor(out=y[i][:], in0=x[i][:], in1=base_t[:, cols], op=ALU.add)

from contextlib import ExitStack

import concourse.mybir as mybir

K, R, F, T, J, U = 512, 128, 512, 2048, 512, 1024
FLOPS = 5 * 2 * 512 * R * J

F32 = mybir.dt.float32
BF16 = mybir.dt.bfloat16
I32 = mybir.dt.int32
U32 = mybir.dt.uint32
U16 = mybir.dt.uint16
U8 = mybir.dt.uint8
FP8X4 = mybir.dt.float8_e4m3fn_x4
ALU = mybir.AluOpType
ACT = mybir.ActivationFunctionType

P = 128
PACK = 4
HALF = J // 2
DTAB_ROW = 4


def interleave(engine_copy, grouped, raw):
    engine_copy(
        out=grouped.rearrange("p (c i t) -> p c t i", i=4, t=PACK),
        in_=raw.rearrange("p t (c i) -> p c t i", i=4),
    )


def tile_attend_hvcarrymix_kernel(tc, tab_words, tab_scales, w1, w2, bias, carry, wo, dy, dtab_words, dtab_scales, og, base, offs, offs2, out):
    nc = tc.nc
    with ExitStack() as ctx:
        sb = ctx.enter_context(tc.tile_pool(name="sb", bufs=1))
        ps = ctx.enter_context(tc.psum_pool(name="ps", bufs=1))

        def tile(name, shape, dtype, tag=None):
            return sb.tile(shape, dtype, name=name, tag=tag or name, align_bytes=64)

        offs_t = tile("offs_t", [P, J // 16], U16)
        offs2_t = tile("offs2_t", [P, J // 16], U16)
        tab_s = tile("tab_s", [P, T], U8)
        w1_raw = tile("w1_raw", [P, PACK, R], F32)
        w2_raw = tile("w2_raw", [P, PACK, R], F32)
        carry_t = tile("carry_t", [P, U], F32)
        bias_t = tile("bias_t", [P, 1], F32)
        og_t = tile("og_t", [P, 1], F32)

        nc.vector.memset(tab_s[:].bitcast(I32), 0)

        def words(ap):
            return ap[0].rearrange("p n t -> p (n t)").bitcast(I32)

        def k_rows(ap):
            return ap.rearrange("(p t) c -> p t c", t=PACK)

        def load_scales(queue, plane, first_row, scales):
            rows = scales[0].bitcast(I32).rearrange("(q r) n -> r q n", r=4)
            for r in range(4):
                queue.dma_start(out=plane[first_row + r : P : 32, :].bitcast(I32), in_=rows[r])

        nc.scalar.dma_start(out=bias_t[:], in_=bias)
        nc.scalar.dma_start(out=og_t[:], in_=og)
        nc.sync.dma_start(offs2_t[:], offs2)
        nc.sync.dma_start(offs_t[:], offs)
        nc.sync.dma_start(out=carry_t[:], in_=carry)
        nc.sync.dma_start(out=w1_raw[:], in_=k_rows(w1))
        nc.sync.dma_start(out=w2_raw[:], in_=k_rows(w2))
        load_scales(nc.sync, tab_s, 0, tab_scales)

        half_bias = tile("half_bias", [P, 1], F32, tag="shared")
        gain = tile("gain", [P, 1], F32)
        nc.vector.tensor_scalar(out=half_bias[:], in0=bias_t[:], scalar1=0.5, scalar2=None, op0=ALU.mult)
        nc.vector.tensor_scalar(out=gain[:], in0=og_t[:], scalar1=0.25, scalar2=None, op0=ALU.mult)
        tab_w = tile("tab_w", [P, T], U32, tag="bias_t")
        nc.sync.dma_start(out=tab_w[:].bitcast(I32), in_=words(tab_words))
        dtab_s = tile("dtab_s", [P, T], U8, tag="og_t")
        nc.vector.memset(dtab_s[:].bitcast(I32), 0)
        load_scales(nc.sync, dtab_s, DTAB_ROW, dtab_scales)

        carry_g = tile("carry_g", [P, J], F32)
        nc.vector.tensor_copy(out=carry_g[:], in_=carry_t[:].indirect(offs2_t[:]))
        tab_gs = tile("tab_gs", [P, J], U8, tag="carry_t")
        tab_gw = tile("tab_gw", [P, J], U32)
        nc.vector.tensor_copy(out=tab_gs[:], in_=tab_s[:].indirect(offs_t[:]))

        w12_bf = tile("w12_bf", [P, 2 * R * PACK], BF16)
        w12_q = tile("w12_q", [P, 2 * R], U32, tag="tab_s")
        w12_s = tile("w12_s", [P, 2 * R], U8)
        interleave(nc.scalar.copy, w12_bf[:, : R * PACK], w1_raw[:])
        wo_raw = tile("wo_raw", [P, PACK, R], F32, tag="w1_raw")
        nc.sync.dma_start(out=wo_raw[:], in_=k_rows(wo))
        interleave(nc.scalar.copy, w12_bf[:, R * PACK :], w2_raw[:])
        dtab_w = tile("dtab_w", [P, T], U32, tag="w2_raw")
        nc.sync.dma_start(out=dtab_w[:].bitcast(I32), in_=words(dtab_words))
        nc.vector.quantize_mx(out=w12_q[:].bitcast(FP8X4), scales=w12_s[:], in_=w12_bf[:])


        late_raw = tile("late_raw", [P, J * PACK + J], F32, tag="w12_bf")
        dy_raw = [late_raw[:, i * HALF * PACK : (i + 1) * HALF * PACK].rearrange("p (t c) -> p t c", t=PACK) for i in range(2)]
        base_t = late_raw[:, J * PACK :]
        wo_bf = tile("wo_bf", [P, R * PACK], BF16)
        interleave(nc.scalar.copy, wo_bf[:], wo_raw[:])
        for i in range(2):
            nc.sync.dma_start(out=dy_raw[i], in_=k_rows(dy)[:, :, i * HALF : (i + 1) * HALF])
        nc.sync.dma_start(out=base_t, in_=base)

        nc.vector.tensor_copy(out=tab_gw[:], in_=tab_w[:].indirect(offs_t[:]))
        dtab_gs = tile("dtab_gs", [P, J], U8, tag="bias_t")
        nc.vector.tensor_copy(out=dtab_gs[:], in_=dtab_s[:].indirect(offs_t[:]))

        def product(acc, lhs_q, lhs_s, rhs_q, rhs_s):
            nc.tensor.matmul_mx(out=acc, lhsT=lhs_q.bitcast(FP8X4), lhsT_scale=lhs_s, rhs=rhs_q.bitcast(FP8X4), rhs_scale=rhs_s, start=True, stop=True)

        a_ps = ps.tile([P, J], F32, name="a_ps")
        b_ps = ps.tile([P, J], F32, name="b_ps")
        ta_ps = ps.tile([P, J], F32, name="ta_ps")
        tb_ps = ps.tile([P, J], F32, name="tb_ps")
        product(a_ps[:], w12_q[:, :R], w12_s[:, :R], tab_gw[:], tab_gs[:])
        product(b_ps[:], w12_q[:, R:], w12_s[:, R:], tab_gw[:], tab_gs[:])

        h = tile("h", [P, J], F32)
        t = tile("t", [P, J], F32)
        h2 = tile("h2", [P, J], F32)
        nc.scalar.activation(out=h[:], in_=a_ps[:], func=ACT.Tanh)
        nc.scalar.activation(out=t[:], in_=b_ps[:], func=ACT.Tanh, bias=half_bias[:], scale=0.5)
        nc.scalar.activation(out=h2[:], in_=h[:], func=ACT.Square)
        t2 = tile("t2", [P, J], F32)
        nc.scalar.activation(out=t2[:], in_=t[:], func=ACT.Square)

        u = tile("u", [P, J], F32)
        f = tile("f", [P, J], F32)
        dtab_gw = tile("dtab_gw", [P, J], U32, tag="og_t")
        nc.vector.tensor_copy(out=dtab_gw[:], in_=dtab_w[:].indirect(offs_t[:]))
        product(ta_ps[:], w12_q[:, :R], w12_s[:, :R], dtab_gw[:], dtab_gs[DTAB_ROW:P, :])
        product(tb_ps[:], w12_q[:, R:], w12_s[:, R:], dtab_gw[:], dtab_gs[DTAB_ROW:P, :])
        d = tile("d", [P, J], F32)
        e = tile("e", [P, J], F32, tag="w2_raw")
        nc.gpsimd.tensor_tensor(out=d[:], in0=carry_g[:], in1=h[:], op=ALU.subtract)
        nc.vector.tensor_tensor(out=e[:], in0=d[:], in1=t[:], op=ALU.mult)
        nc.vector.scalar_tensor_tensor(out=u[:], in0=h2[:], scalar=-1.0, in1=ta_ps[:], op0=ALU.add, op1=ALU.mult)

        late_bf = tile("late_bf", [P, J * PACK], BF16, tag="shared")
        wo_q = tile("wo_q", [P, R], U32, tag="d")
        wo_s = tile("wo_s", [P, R], U8)
        nc.vector.quantize_mx(out=wo_q[:].bitcast(FP8X4), scales=wo_s[:], in_=wo_bf[:])

        nc.vector.tensor_tensor(out=f[:], in0=e[:], in1=tb_ps[:], op=ALU.mult)

        c_ps = []
        for i in range(2):
            dy_bf = late_bf[:, i * HALF * PACK : (i + 1) * HALF * PACK]
            dy_q = tile("dy_q%d" % i, [P, HALF], U32)
            dy_s = tile("dy_s%d" % i, [P, HALF], U8)
            interleave(nc.scalar.copy, dy_bf, dy_raw[i])
            nc.vector.quantize_mx(out=dy_q[:].bitcast(FP8X4), scales=dy_s[:], in_=dy_bf)
            acc = ps.tile([P, HALF], F32, name="c_ps%d" % i)
            product(acc[:], wo_q[:], wo_s[:], dy_q[:], dy_s[:])
            c_ps.append(acc)
            if i == 0:
                v = dy_bf.bitcast(F32)
                nc.vector.tensor_tensor(out=v, in0=u[:], in1=f[:], op=ALU.subtract)
            else:
                z = dy_bf.bitcast(F32)

        for i in range(2):
            cols = slice(i * HALF, (i + 1) * HALF)
            nc.vector.scalar_tensor_tensor(out=z[:, cols], in0=t2[:, cols], scalar=-1.0, in1=v[:, cols], op0=ALU.add, op1=ALU.mult)
        x = [tile("x%d" % i, [P, HALF], F32) for i in range(2)]
        y = [tile("y%d" % i, [P, HALF], F32) for i in range(2)]
        for i in range(2):
            cols = slice(i * HALF, (i + 1) * HALF)
            nc.vector.scalar_tensor_tensor(out=x[i][:], in0=c_ps[i][:], scalar=gain[:], in1=z[:, cols], op0=ALU.mult, op1=ALU.mult)
        for i in range(2):
            cols = slice(i * HALF, (i + 1) * HALF)
            nc.vector.tensor_tensor(out=y[i][:], in0=x[i][:], in1=base_t[:, cols], op=ALU.add)
            nc.sync.dma_start(out=out[:, cols], in_=y[i][:])
